import numpy as np
import ml_dtypes


def mxq(x, axis, fmt="e4m3"):
    dtype, down = {"e4m3": (ml_dtypes.float8_e4m3fn, 7), "e5m2": (ml_dtypes.float8_e5m2, 14)}[fmt]
    v = np.moveaxis(np.asarray(x, np.float32).astype(ml_dtypes.bfloat16).astype(np.float64), axis, -1)
    blocks = v.reshape(v.shape[:-1] + (-1, 32))
    amax = np.abs(blocks).max(-1, keepdims=True)
    byte = np.maximum(np.where(amax > 0, np.frexp(amax)[1] - 1 + 127, 0) - down, 1)
    scale = np.exp2(byte - 127.0)
    codes = (blocks / scale).astype(np.float32).astype(dtype).astype(np.float64)
    return np.moveaxis((codes * scale).reshape(v.shape), -1, axis)


WIDE = False


def mx_kscale(k):
    if not WIDE:
        return np.ones(k)
    levels = np.array([10, -10, 5, -5, 0])
    if k % 512:
        return np.exp2(np.random.permutation(np.resize(levels, k // 32))).repeat(32)
    a = np.empty((k // 512, 16))
    for p in range(k // 512):
        a[p, :8] = np.random.permutation(np.resize(levels, 8))
        for g in range(8):
            far = levels[np.abs(levels - a[p, g]) >= 10]
            a[p, g + 8] = far[np.random.randint(len(far))]
    return np.exp2(a.ravel()).repeat(32)


BF16 = ml_dtypes.bfloat16


def bf(x):
    return np.asarray(x, np.float32).astype(BF16)


def f64(x):
    return np.asarray(x).astype(np.float64)

def planes(Y):
    n, m = Y.shape
    b = f64(bf(Y)).reshape(n // 32, 32, m)
    amax = np.abs(b).max(1)
    byte = np.clip(np.where(amax > 0, np.frexp(amax)[1] - 1 + 127 - 7, 1), 1, 254)
    codes = (b * np.exp2(127.0 - byte)[:, None, :]).reshape(n, m).astype(np.float32).astype(ml_dtypes.float8_e4m3fn).view(np.uint8)
    words = codes.reshape(n // 512, 128, 4, m).transpose(0, 1, 3, 2)
    return np.ascontiguousarray(words), np.ascontiguousarray(byte.astype(np.uint8).reshape(n // 512, 16, m))


N, D, F = 1024, 1024, 1536


def setup_inputs():
    s, t = mx_kscale(D), mx_kscale(F)
    return {
        "p": bf(np.random.standard_normal((N, D))),
        "q": bf(np.random.standard_normal((N, D))),
        "k": bf(np.random.standard_normal((D, F)) / np.sqrt(D) / s[:, None] * t[None, :]),
        "d": bf((1.0 + 0.1 * np.random.standard_normal(D)) * s),
        "e": bf((1.0 + 0.1 * np.random.standard_normal(F)) / t),
        "b": bf(0.4 * np.random.standard_normal(F)),
        "a": bf((1.0 + 0.1 * np.random.standard_normal(F)) / t),
    }


def core(p, q, k, d, e, b, a):
    p, q, k, d, e, b, a = f64(p), f64(q), f64(k), f64(d), f64(e), f64(b), f64(a)
    u = q * d[None, :]
    h = mxq(u, 1, "e4m3") @ mxq(k, 0, "e4m3")
    th = np.tanh(e[None, :] * h + b[None, :])
    g = a[None, :] * th
    r = mxq(g, 1, "e4m3") @ mxq(k.T, 0, "e4m3")
    return p + d[None, :] * r


def reference(p, q, k, d, e, b, a):
    R_out = core(p, q, k, d, e, b, a)
    words, scales = planes(R_out)
    return R_out, words, scales

@@ -1,0 +1,453 @@
+from contextlib import ExitStack
+
+import concourse.mybir as mybir
+from concourse.masks import make_identity
+
+N, D, F = 1024, 1024, 1536
+FLOPS = 2 * 2 * N * D * F
+
+F32 = mybir.dt.float32
+BF16 = mybir.dt.bfloat16
+I32 = mybir.dt.int32
+U32 = mybir.dt.uint32
+U8 = mybir.dt.uint8
+FP8X4 = mybir.dt.float8_e4m3fn_x4
+ACT = mybir.ActivationFunctionType
+ALU = mybir.AluOpType
+
+P = 128
+TG = 2
+GD = 2
+GF = 3
+W = 512
+
+
+def tile_sympnetgradientshearblock_x1_kernel(tc, p, q, k, d, e, b, a, out, out_words, out_scales):
+    nc = tc.nc
+    ctx = ExitStack()
+    with ctx:
+        keep = ctx.enter_context(tc.tile_pool(name="keep", bufs=1))
+        grp_pool = ctx.enter_context(tc.tile_pool(name="grp", bufs=8))
+        th_pool = ctx.enter_context(tc.tile_pool(name="th", bufs=2))
+        o_pool = ctx.enter_context(tc.tile_pool(name="o", bufs=3))
+        oc_pool = ctx.enter_context(tc.tile_pool(name="oc", bufs=3))
+        rt_pool = ctx.enter_context(tc.tile_pool(name="rt", bufs=4))
+        tr_psum = ctx.enter_context(tc.psum_pool(name="trp", bufs=3))
+        acc_psum = ctx.enter_context(tc.psum_pool(name="accp", bufs=8 - 3))
+        if True:
+            ctx.enter_context(tc.manual_schedule())
+
+        q4 = q.rearrange("(g m t) x -> g m t x", g=TG, t=4)
+        p4 = p.rearrange("(g m t) x -> g m t x", g=TG, t=4)
+        out4 = out.rearrange("(g m t) x -> g m t x", g=TG, t=4)
+        k4 = k.rearrange("(g m j) f -> g m j f", g=GD, j=4)
+
+        vec = keep.tile([P, W], BF16, name="vec", align_bytes=64)
+        nc.gpsimd.memset(vec[:], 0.0)
+        warm = keep.tile([P, 1], F32, name="warm")
+        nc.vector.memset(warm[:], 0.0)
+        ident32 = keep.tile([P, P], F32, name="ident32", align_bytes=64)
+        make_identity(nc, ident32[:])
+        ident16 = keep.tile([P, P], BF16, name="ident16", align_bytes=64)
+        nc.vector.tensor_copy(out=ident16[:], in_=ident32[:])
+
+        q_sb, k_sb, p_sb = {}, {}, {}
+
+        def load_q(g, t):
+            q_sb[g, t] = keep.tile([P, D], BF16, name="q%d%d" % (g, t), align_bytes=64)
+            nc.sync.dma_start(out=q_sb[g, t][:], in_=q4[g, :, t, :])
+
+        def load_k(gd, gf):
+            k_sb[gd, gf] = keep.tile([P, 4, W], BF16, name="k%d%d" % (gd, gf), align_bytes=64)
+            nc.sync.dma_start(out=k_sb[gd, gf][:], in_=k4[gd, :, :, gf * W : (gf + 1) * W])
+
+        def load_p(g):
+            p_sb[g] = keep.tile([P, 4, D], BF16, name="p%d" % g, align_bytes=64)
+            nc.sync.dma_start(out=p_sb[g][:], in_=p4[g])
+
+        load_q(0, 0)
+        load_k(0, 0)
+        for row, (v, n) in ((9, (d, GD)), (0, (e, GF)), (3, (b, GF)), (6, (a, GF))):
+            nc.sync.dma_start(out=vec[row : row + n, :], in_=v.rearrange("(g x) -> g x", g=n))
+        load_q(0, 1)
+        load_q(0, 2)
+        load_q(0, 3)
+        load_k(1, 0)
+        load_k(0, 1)
+        load_k(1, 1)
+        for t in range(4):
+            load_q(1, t)
+        load_k(0, 2)
+        load_k(1, 2)
+        load_p(0)
+        load_p(1)
+
+        nc.scalar.activation(warm[:], warm[:], ACT.Tanh)
+
+        eb = keep.tile([P, 4, 6], F32, name="eb")
+        a4 = keep.tile([P, GF, 4], F32, name="a4")
+        d4 = keep.tile([P, GD, 4], BF16, name="d4")
+
+        vps = {}
+
+        def vectors():
+            ps = tr_psum.tile([P, 4, P], BF16, name="vps", tag="tr")
+            for t in range(4):
+                nc.tensor.transpose(ps[:, t, :], vec[:, t : W : 4], ident16[:])
+            vps[0] = ps
+
+        def vec_cp():
+            ps = vps[0]
+            nc.vector.tensor_copy(out=d4[:], in_=ps[:, :, 9:11].rearrange("p t g -> p g t"))
+            nc.vector.tensor_copy(out=eb[:], in_=ps[:, :, 0:6])
+            nc.vector.tensor_copy(out=a4[:], in_=ps[:, :, 6:9].rearrange("p t g -> p g t"))
+
+        d_col = keep.tile([P, 8], F32, name="d_col")
+
+        def dcol():
+            ps = tr_psum.tile([P, 4, P], BF16, name="dps", tag="tr")
+            for s in range(4):
+                nc.tensor.transpose(ps[:, s, :], vec[:, s * P : (s + 1) * P], ident16[:])
+            vps[1] = ps
+
+        def dcol_cp():
+            ps = vps[1]
+            nc.vector.tensor_copy(out=d_col[:].rearrange("p (g s) -> p g s", g=GD), in_=ps[:, :, 9:11].rearrange("p s g -> p g s"))
+
+        ug, uc, us = {}, {}, {}
+
+        ubank = {}
+
+        def u_tr(g, pair):
+            for gd in range(GD):
+                if pair == 0:
+                    ug[g, gd] = grp_pool.tile([P, W, 4], BF16, name="ug", tag="grp", align_bytes=64)
+                bank = ubank[g, pair, gd] = tr_psum.tile([P, 2, 2, P], F32, name="ubank", tag="tr")
+                for u in range(2):
+                    for tt in range(2):
+                        words = q_sb[g, 2 * pair + tt][:].bitcast(F32)
+                        nc.tensor.transpose(bank[:, u, tt, :], words[:, 256 * gd + u : 256 * (gd + 1) : 2], ident32[:])
+
+        def u_mul(g, pair):
+            for gd in range(GD):
+                bank = ubank[g, pair, gd]
+                nc.vector.tensor_tensor(
+                    out=ug[g, gd][:, 256 * pair : 256 * (pair + 1), :].rearrange("p n (u e) -> p n u e", e=2),
+                    in0=bank[:].rearrange("p u t m -> p (u t m)").bitcast(BF16).rearrange("p (u n e) -> p n u e", u=2, e=2),
+                    in1=d4[:, gd, :].rearrange("p (u e) -> p u e", e=2).unsqueeze(1).to_broadcast([P, 256, 2, 2]),
+                    op=ALU.mult,
+                )
+
+        def quant(src, name):
+            codes = keep.tile([P, W], U32, name=name + "c", align_bytes=64)
+            scales = keep.tile([P, W], U8, name=name + "s", align_bytes=64)
+            nc.vector.quantize_mx(out=codes[:].bitcast(FP8X4), scales=scales[:], in_=src[:].rearrange("p n t -> p (n t)"))
+            return codes, scales
+
+        def u_q(g, gd):
+            uc[g, gd], us[g, gd] = quant(ug[g, gd], "u%d%d" % (g, gd))
+
+        kg, kc, ks = {}, {}, {}
+
+        def k_il(gd, gf, eng):
+            kg[gd, gf] = grp_pool.tile([P, W, 4], BF16, name="kg", tag="grp", align_bytes=64)
+            dst = kg[gd, gf][:].rearrange("p (t m) j -> p t m j", t=4)
+            src = k_sb[gd, gf][:].rearrange("p j (m t) -> p t m j", t=4)
+            if eng == "V":
+                nc.vector.tensor_copy(out=dst, in_=src)
+            else:
+                nc.scalar.copy(dst, src)
+
+        def k_q(gd, gf):
+            kc[gd, gf], ks[gd, gf] = quant(kg[gd, gf], "k%d%d" % (gd, gf))
+
+        ktg, ktc, kts = {}, {}, {}
+
+        kbank = {}
+
+        def kt_tr(gd, gf):
+            for jj in range(2):
+                bank = kbank[gd, gf, jj] = tr_psum.tile([P, 2, 2, P], F32, name="kbank", tag="tr")
+                for j in range(2):
+                    words = k_sb[gd, gf][:, 2 * jj + j, :].bitcast(F32)
+                    for u in range(2):
+                        nc.tensor.transpose(bank[:, j, u, :], words[:, u : 256 : 2], ident32[:])
+
+        def kt_cp(gd, gf, eng="S"):
+            ktg[gd, gf] = grp_pool.tile([P, W, 4], BF16, name="ktg", tag="grp", align_bytes=64)
+            dst = ktg[gd, gf][:].rearrange("p n t -> p (n t)").bitcast(F32).rearrange("p (m j u) -> p m j u", j=4, u=2)
+            for jj in range(2):
+                src = kbank[gd, gf, jj][:].rearrange("p j u m -> p m j u")
+                if eng == "S":
+                    nc.scalar.copy(dst[:, :, 2 * jj : 2 * jj + 2, :], src)
+                else:
+                    nc.vector.tensor_copy(out=dst[:, :, 2 * jj : 2 * jj + 2, :], in_=src)
+
+        def kt_q(gd, gf):
+            ktc[gd, gf], kts[gd, gf] = quant(ktg[gd, gf], "kt%d%d" % (gd, gf))
+
+        th, gg, gc, gs = {}, {}, {}, {}
+
+        acc1 = {}
+
+        def mm1(g, gf):
+            for t in range(4):
+                acc = acc1[g, gf, t] = acc_psum.tile([P, W], F32, name="acc1", tag="acc")
+                cols = slice(t * P, (t + 1) * P)
+                for gd in range(GD):
+                    nc.tensor.matmul_mx(
+                        out=acc[:],
+                        lhsT=kc[gd, gf][:, cols].bitcast(FP8X4),
+                        lhsT_scale=ks[gd, gf][:, cols],
+                        rhs=uc[g, gd][:].bitcast(FP8X4),
+                        rhs_scale=us[g, gd][:],
+                        start=(gd == 0),
+                        stop=(gd == GD - 1),
+                    )
+
+        def tanh(g, gf):
+            th[g, gf] = th_pool.tile([P, 4, W], F32, name="th", tag="th", align_bytes=64)
+            for t in range(4):
+                acc = acc1[g, gf, t]
+                nc.scalar.activation(
+                    th[g, gf][:, t, :], acc[:], ACT.Tanh, bias=eb[:, t, 3 + gf : 4 + gf], scale=eb[:, t, gf : gf + 1]
+                )
+
+        def am(g, gf):
+            gg[g, gf] = grp_pool.tile([P, W, 4], BF16, name="gg", tag="grp", align_bytes=64)
+            nc.vector.tensor_tensor(
+                out=gg[g, gf][:],
+                in0=th[g, gf][:].rearrange("p t n -> p n t"),
+                in1=a4[:, gf, :].unsqueeze(1).to_broadcast([P, W, 4]),
+                op=ALU.mult,
+            )
+
+        def gq(g, gf):
+            gc[g, gf], gs[g, gf] = quant(gg[g, gf], "g%d%d" % (g, gf))
+
+        ot, ob, oc, osc = {}, {}, {}, {}
+
+        rt, acc2, rbank = {}, {}, {}
+
+        def mm2(g, n, s):
+            acc = acc2[g, n, s] = acc_psum.tile([P, W], F32, name="acc2", tag="acc")
+            cols = slice(s * P, (s + 1) * P)
+            for gf in range(GF):
+                nc.tensor.matmul_mx(
+                    out=acc[:],
+                    lhsT=ktc[n, gf][:, cols].bitcast(FP8X4),
+                    lhsT_scale=kts[n, gf][:, cols],
+                    rhs=gc[g, gf][:].bitcast(FP8X4),
+                    rhs_scale=gs[g, gf][:],
+                    start=(gf == 0),
+                    stop=(gf == GF - 1),
+                )
+
+        def rd(g, n, s):
+            acc = acc2[g, n, s]
+            rt[g, n, s] = rt_pool.tile([P, W], F32, name="rt", tag="rt", align_bytes=64)
+            nc.scalar.activation(rt[g, n, s][:], acc[:], ACT.Copy, scale=d_col[:, n * 4 + s : n * 4 + s + 1])
+
+        def rtr(g, n, s):
+            bank = rbank[g, n, s] = tr_psum.tile([P, 4, P], F32, name="rbank", tag="tr")
+            for t in range(4):
+                nc.tensor.transpose(bank[:, t, :], rt[g, n, s][:, t * P : (t + 1) * P], ident32[:])
+
+        def add(g, n, s):
+            if s == 0:
+                ot[g, n] = o_pool.tile([P, 4, W], F32, name="ot", tag="ot", align_bytes=64)
+            bank = rbank[g, n, s]
+            c0 = n * W + s * P
+            nc.vector.tensor_tensor(
+                out=ot[g, n][:, :, s * P : (s + 1) * P], in0=bank[:], in1=p_sb[g][:, :, c0 : c0 + P], op=ALU.add
+            )
+
+        def ob_(g, n, c0, c1, eng="S"):
+            if (g, n) not in ob:
+                ob[g, n] = grp_pool.tile([P, W, 4], BF16, name="ob", tag="grp", align_bytes=64)
+            dst = ob[g, n][:, c0:c1, :]
+            src = ot[g, n][:, :, c0:c1].rearrange("p t n -> p n t")
+            if eng == "S":
+                nc.scalar.copy(dst, src)
+            else:
+                nc.vector.tensor_copy(out=dst, in_=src)
+
+        def oq(g, n, c0, c1):
+            if (g, n) not in oc:
+                oc[g, n] = oc_pool.tile([P, W], U32, name="oc", tag="oc", align_bytes=64)
+                if g not in osc:
+                    osc[g] = keep.tile([P, D], U8, name="osc%d" % g, align_bytes=64)
+            nc.vector.quantize_mx(
+                out=oc[g, n][:, c0:c1].bitcast(FP8X4),
+                scales=osc[g][:, n * W + c0 : n * W + c1],
+                in_=ob[g, n][:, c0:c1, :].rearrange("p n t -> p (n t)"),
+            )
+
+        def st_o(g, n):
+            nc.sync.dma_start(out=out4[g, :, :, n * W : (n + 1) * W], in_=ot[g, n][:])
+
+        def st_w(g, n, c0, c1):
+            nc.sync.dma_start(
+                out=out_words[g, :, n * W + c0 : n * W + c1, :].rearrange("p m t -> p (m t)").bitcast(I32),
+                in_=oc[g, n][:, c0:c1].bitcast(I32),
+            )
+
+        def st_s(g):
+            for qd in range(4):
+                nc.sync.dma_start(
+                    out=out_scales[g, 4 * qd : 4 * qd + 4, :].bitcast(I32), in_=osc[g][32 * qd : 32 * qd + 4, :].bitcast(I32)
+                )
+        vectors()
+        vec_cp()
+        k_il(0, 0, "S")
+        u_tr(0, 0)
+        u_mul(0, 0)
+        u_tr(0, 1)
+        u_mul(0, 1)
+        u_q(0, 0)
+        u_q(0, 1)
+        kt_tr(0, 0)
+        kt_cp(0, 0)
+        k_il(1, 0, "S")
+        k_il(0, 1, "V")
+        k_il(1, 1, "S")
+        k_q(0, 0)
+        k_q(1, 0)
+        u_tr(1, 0)
+        u_mul(1, 0)
+        mm1(0, 0)
+        kt_q(0, 0)
+        k_q(0, 1)
+        k_q(1, 1)
+        k_il(0, 2, "V")
+        tanh(0, 0)
+        k_il(1, 2, "S")
+        u_tr(1, 1)
+        u_mul(1, 1)
+        mm1(0, 1)
+        u_q(1, 0)
+        k_q(0, 2)
+        k_q(1, 2)
+        tanh(0, 1)
+        am(0, 0)
+        kt_tr(0, 1)
+        kt_cp(0, 1)
+        u_q(1, 1)
+        mm1(0, 2)
+        am(0, 1)
+        gq(0, 0)
+        tanh(0, 2)
+        kt_tr(0, 2)
+        kt_cp(0, 2)
+        gq(0, 1)
+        kt_q(0, 1)
+        am(0, 2)
+        mm1(1, 0)
+        kt_q(0, 2)
+        gq(0, 2)
+        kt_tr(1, 0)
+        kt_cp(1, 0)
+        kt_tr(1, 1)
+        kt_cp(1, 1)
+        kt_q(1, 0)
+        tanh(1, 0)
+        dcol()
+        kt_tr(1, 2)
+        dcol_cp()
+        kt_q(1, 1)
+        kt_cp(1, 2)
+        am(1, 0)
+        kt_q(1, 2)
+        gq(1, 0)
+        mm2(0, 0, 0)
+        rd(0, 0, 0)
+        mm2(0, 0, 1)
+        rd(0, 0, 1)
+        mm2(0, 0, 2)
+        rd(0, 0, 2)
+        mm2(0, 0, 3)
+        rd(0, 0, 3)
+        mm1(1, 1)
+        tanh(1, 1)
+        rtr(0, 0, 0)
+        add(0, 0, 0)
+        rtr(0, 0, 1)
+        add(0, 0, 1)
+        mm1(1, 2)
+        am(1, 1)
+        tanh(1, 2)
+        rtr(0, 0, 2)
+        add(0, 0, 2)
+        rtr(0, 0, 3)
+        add(0, 0, 3)
+        st_o(0, 0)
+        gq(1, 1)
+        mm2(0, 1, 0)
+        rd(0, 1, 0)
+        mm2(0, 1, 1)
+        rd(0, 1, 1)
+        mm2(0, 1, 2)
+        rd(0, 1, 2)
+        mm2(0, 1, 3)
+        rd(0, 1, 3)
+        am(1, 2)
+        ob_(0, 0, 0, 512)
+        gq(1, 2)
+        rtr(0, 1, 0)
+        add(0, 1, 0)
+        rtr(0, 1, 1)
+        add(0, 1, 1)
+        rtr(0, 1, 2)
+        add(0, 1, 2)
+        rtr(0, 1, 3)
+        add(0, 1, 3)
+        st_o(0, 1)
+        oq(0, 0, 0, 512)
+        st_w(0, 0, 0, 512)
+        mm2(1, 0, 0)
+        rd(1, 0, 0)
+        mm2(1, 0, 1)
+        rd(1, 0, 1)
+        mm2(1, 0, 2)
+        rd(1, 0, 2)
+        mm2(1, 0, 3)
+        rd(1, 0, 3)
+        ob_(0, 1, 0, 512)
+        rtr(1, 0, 0)
+        add(1, 0, 0)
+        rtr(1, 0, 1)
+        add(1, 0, 1)
+        rtr(1, 0, 2)
+        add(1, 0, 2)
+        rtr(1, 0, 3)
+        add(1, 0, 3)
+        st_o(1, 0)
+        oq(0, 1, 0, 512)
+        st_w(0, 1, 0, 512)
+        st_s(0)
+        mm2(1, 1, 0)
+        rd(1, 1, 0)
+        mm2(1, 1, 1)
+        rd(1, 1, 1)
+        mm2(1, 1, 2)
+        rd(1, 1, 2)
+        mm2(1, 1, 3)
+        rd(1, 1, 3)
+        ob_(1, 0, 0, 512)
+        rtr(1, 1, 0)
+        add(1, 1, 0)
+        rtr(1, 1, 1)
+        add(1, 1, 1)
+        rtr(1, 1, 2)
+        add(1, 1, 2)
+        rtr(1, 1, 3)
+        add(1, 1, 3)
+        st_o(1, 1)
+        oq(1, 0, 0, 512)
+        st_w(1, 0, 0, 512)
+        ob_(1, 1, 0, 256)
+        ob_(1, 1, 256, 512, "V")
+        oq(1, 1, 256, 512)
+        oq(1, 1, 0, 256)
+        st_w(1, 1, 0, 512)
+        st_s(1)

@@ -20,6 +20,7 @@ TG = 2
 GD = 2
 GF = 3
 W = 512
+PAIR = 2
 
 
 def tile_sympnetgradientshearblock_x1_kernel(tc, p, q, k, d, e, b, a, out, out_words, out_scales):
@@ -27,10 +28,12 @@ def tile_sympnetgradientshearblock_x1_kernel(tc, p, q, k, d, e, b, a, out, out_w
     ctx = ExitStack()
     with ctx:
         keep = ctx.enter_context(tc.tile_pool(name="keep", bufs=1))
-        grp_pool = ctx.enter_context(tc.tile_pool(name="grp", bufs=8))
+        grp_pool = ctx.enter_context(tc.tile_pool(name="grp", bufs=5))
+        grp2_pool = ctx.enter_context(tc.tile_pool(name="grp2", bufs=4))
         th_pool = ctx.enter_context(tc.tile_pool(name="th", bufs=2))
         o_pool = ctx.enter_context(tc.tile_pool(name="o", bufs=3))
         oc_pool = ctx.enter_context(tc.tile_pool(name="oc", bufs=3))
+        t1_pool = ctx.enter_context(tc.tile_pool(name="t1", bufs=2))
         rt_pool = ctx.enter_context(tc.tile_pool(name="rt", bufs=4))
         tr_psum = ctx.enter_context(tc.psum_pool(name="trp", bufs=3))
         acc_psum = ctx.enter_context(tc.psum_pool(name="accp", bufs=8 - 3))
@@ -53,39 +56,38 @@ def tile_sympnetgradientshearblock_x1_kernel(tc, p, q, k, d, e, b, a, out, out_w
 
         q_sb, k_sb, p_sb = {}, {}, {}
 
-        def load_q(g, t):
-            q_sb[g, t] = keep.tile([P, D], BF16, name="q%d%d" % (g, t), align_bytes=64)
-            nc.sync.dma_start(out=q_sb[g, t][:], in_=q4[g, :, t, :])
+        def load_q(g, t0, t1):
+            tile = keep.tile([P, t1 - t0, D], BF16, name="q%d%d" % (g, t0), align_bytes=64)
+            nc.sync.dma_start(out=tile[:], in_=q4[g, :, t0:t1, :])
+            for t in range(t0, t1):
+                q_sb[g, t] = tile[:, t - t0, :]
 
-        def load_k(gd, gf):
-            k_sb[gd, gf] = keep.tile([P, 4, W], BF16, name="k%d%d" % (gd, gf), align_bytes=64)
-            nc.sync.dma_start(out=k_sb[gd, gf][:], in_=k4[gd, :, :, gf * W : (gf + 1) * W])
+        def load_k(gd, f0, f1):
+            tile = keep.tile([P, 4, (f1 - f0) * W], BF16, name="k%d%d" % (gd, f0), align_bytes=64)
+            nc.sync.dma_start(out=tile[:], in_=k4[gd, :, :, f0 * W : f1 * W])
+            for gf in range(f0, f1):
+                k_sb[gd, gf] = tile[:, :, (gf - f0) * W : (gf - f0 + 1) * W]
 
         def load_p(g):
             p_sb[g] = keep.tile([P, 4, D], BF16, name="p%d" % g, align_bytes=64)
             nc.sync.dma_start(out=p_sb[g][:], in_=p4[g])
 
-        load_q(0, 0)
-        load_k(0, 0)
+        load_k(0, 0, 1)
         for row, (v, n) in ((9, (d, GD)), (0, (e, GF)), (3, (b, GF)), (6, (a, GF))):
             nc.sync.dma_start(out=vec[row : row + n, :], in_=v.rearrange("(g x) -> g x", g=n))
-        load_q(0, 1)
-        load_q(0, 2)
-        load_q(0, 3)
-        load_k(1, 0)
-        load_k(0, 1)
-        load_k(1, 1)
-        for t in range(4):
-            load_q(1, t)
-        load_k(0, 2)
-        load_k(1, 2)
+        load_q(0, 0, 2)
+        load_k(1, 0, 1)
+        load_q(0, 2, 4)
+        load_k(0, 1, 3)
+        load_k(1, 1, 3)
+        load_q(1, 0, 4)
         load_p(0)
         load_p(1)
 
         nc.scalar.activation(warm[:], warm[:], ACT.Tanh)
 
-        eb = keep.tile([P, 4, 6], F32, name="eb")
         a4 = keep.tile([P, GF, 4], F32, name="a4")
+        eb = keep.tile([P, 4, 6], F32, name="eb")
         d4 = keep.tile([P, GD, 4], BF16, name="d4")
 
         vps = {}
@@ -99,10 +101,21 @@ def tile_sympnetgradientshearblock_x1_kernel(tc, p, q, k, d, e, b, a, out, out_w
         def vec_cp():
             ps = vps[0]
             nc.vector.tensor_copy(out=d4[:], in_=ps[:, :, 9:11].rearrange("p t g -> p g t"))
-            nc.vector.tensor_copy(out=eb[:], in_=ps[:, :, 0:6])
             nc.vector.tensor_copy(out=a4[:], in_=ps[:, :, 6:9].rearrange("p t g -> p g t"))
+            nc.vector.tensor_copy(out=eb[:], in_=ps[:, :, 0:6])
 
         d_col = keep.tile([P, 8], F32, name="d_col")
+
+        d_all = keep.tile([P, D], BF16, name="d_all", align_bytes=64)
+
+        def dsp():
+            ps = vps[2] = tr_psum.tile([P, GD, 4, P], BF16, name="dps", tag="tr")
+            for g in range(GD):
+                for t in range(4):
+                    nc.tensor.transpose(ps[:, g, t, :], d4[:, g, t : t + 1].to_broadcast([P, P]), ident16[:])
+
+        def dsp_cp():
+            nc.scalar.copy(d_all[:].rearrange("p (g m t) -> p g m t", g=GD, t=4), vps[2][:].rearrange("p g t m -> p g m t"))
 
         def dcol():
             ps = tr_psum.tile([P, 4, P], BF16, name="dps", tag="tr")
@@ -120,12 +133,15 @@ def tile_sympnetgradientshearblock_x1_kernel(tc, p, q, k, d, e, b, a, out, out_w
 
         def u_tr(g, pair):
             for gd in range(GD):
-                if pair == 0:
-                    ug[g, gd] = grp_pool.tile([P, W, 4], BF16, name="ug", tag="grp", align_bytes=64)
+                if (g, 0) not in ug:
+                    tile = grp2_pool.tile([P, GD, W, 4], BF16, name="ug", tag="grp2", align_bytes=64)
+                    ug[g] = tile
+                    for x in range(GD):
+                        ug[g, x] = tile[:, x, :, :]
                 bank = ubank[g, pair, gd] = tr_psum.tile([P, 2, 2, P], F32, name="ubank", tag="tr")
                 for u in range(2):
                     for tt in range(2):
-                        words = q_sb[g, 2 * pair + tt][:].bitcast(F32)
+                        words = q_sb[g, 2 * pair + tt].bitcast(F32)
                         nc.tensor.transpose(bank[:, u, tt, :], words[:, 256 * gd + u : 256 * (gd + 1) : 2], ident32[:])
 
         def u_mul(g, pair):
@@ -144,22 +160,39 @@ def tile_sympnetgradientshearblock_x1_kernel(tc, p, q, k, d, e, b, a, out, out_w
             nc.vector.quantize_mx(out=codes[:].bitcast(FP8X4), scales=scales[:], in_=src[:].rearrange("p n t -> p (n t)"))
             return codes, scales
 
-        def u_q(g, gd):
-            uc[g, gd], us[g, gd] = quant(ug[g, gd], "u%d%d" % (g, gd))
+        def quant2(src, name):
+            codes = keep.tile([P, GD, W], U32, name=name + "c", align_bytes=64)
+            scales = keep.tile([P, GD, W], U8, name=name + "s", align_bytes=64)
+            nc.vector.quantize_mx(
+                out=codes[:].rearrange("p g n -> p (g n)").bitcast(FP8X4),
+                scales=scales[:].rearrange("p g n -> p (g n)"),
+                in_=src[:].rearrange("p g n t -> p (g n t)"),
+            )
+            return codes, scales
+
+        def u_q(g):
+            codes, scales = quant2(ug[g], "u%d" % g)
+            for gd in range(GD):
+                uc[g, gd], us[g, gd] = codes[:, gd, :], scales[:, gd, :]
 
         kg, kc, ks = {}, {}, {}
 
         def k_il(gd, gf, eng):
-            kg[gd, gf] = grp_pool.tile([P, W, 4], BF16, name="kg", tag="grp", align_bytes=64)
-            dst = kg[gd, gf][:].rearrange("p (t m) j -> p t m j", t=4)
-            src = k_sb[gd, gf][:].rearrange("p j (m t) -> p t m j", t=4)
+            if gf not in kg:
+                kg[gf] = grp2_pool.tile([P, GD, W, 4], BF16, name="kg", tag="grp2", align_bytes=64)
+            dst = kg[gf][:, gd, :, :].rearrange("p (t m) j -> p t m j", t=4)
+            src = k_sb[gd, gf].rearrange("p j (m t) -> p t m j", t=4)
             if eng == "V":
                 nc.vector.tensor_copy(out=dst, in_=src)
+            elif eng == "G":
+                nc.gpsimd.tensor_scalar(out=dst, in0=src, scalar1=1.0, scalar2=0.0, op0=ALU.mult, op1=ALU.add)
             else:
                 nc.scalar.copy(dst, src)
 
-        def k_q(gd, gf):
-            kc[gd, gf], ks[gd, gf] = quant(kg[gd, gf], "k%d%d" % (gd, gf))
+        def k_q(gf):
+            codes, scales = quant2(kg[gf], "k%d" % gf)
+            for gd in range(GD):
+                kc[gd, gf], ks[gd, gf] = codes[:, gd, :], scales[:, gd, :]
 
         ktg, ktc, kts = {}, {}, {}
 
@@ -199,8 +232,8 @@ def tile_sympnetgradientshearblock_x1_kernel(tc, p, q, k, d, e, b, a, out, out_w
                         out=acc[:],
                         lhsT=kc[gd, gf][:, cols].bitcast(FP8X4),
                         lhsT_scale=ks[gd, gf][:, cols],
-                        rhs=uc[g, gd][:].bitcast(FP8X4),
-                        rhs_scale=us[g, gd][:],
+                        rhs=uc[g, gd].bitcast(FP8X4),
+                        rhs_scale=us[g, gd],
                         start=(gd == 0),
                         stop=(gd == GD - 1),
                     )
@@ -216,9 +249,9 @@ def tile_sympnetgradientshearblock_x1_kernel(tc, p, q, k, d, e, b, a, out, out_w
         def am(g, gf):
             gg[g, gf] = grp_pool.tile([P, W, 4], BF16, name="gg", tag="grp", align_bytes=64)
             nc.vector.tensor_tensor(
-                out=gg[g, gf][:],
-                in0=th[g, gf][:].rearrange("p t n -> p n t"),
-                in1=a4[:, gf, :].unsqueeze(1).to_broadcast([P, W, 4]),
+                out=gg[g, gf][:].rearrange("p (c i) t -> p c t i", i=PAIR),
+                in0=th[g, gf][:].rearrange("p t (c i) -> p c t i", i=PAIR),
+                in1=a4[:, gf, :].unsqueeze(1).unsqueeze(3).to_broadcast([P, W // PAIR, 4, PAIR]),
                 op=ALU.mult,
             )
 
@@ -227,7 +260,7 @@ def tile_sympnetgradientshearblock_x1_kernel(tc, p, q, k, d, e, b, a, out, out_w
 
         ot, ob, oc, osc = {}, {}, {}, {}
 
-        rt, acc2, rbank = {}, {}, {}
+        rt, acc2, rbank, t1 = {}, {}, {}, {}
 
         def mm2(g, n, s):
             acc = acc2[g, n, s] = acc_psum.tile([P, W], F32, name="acc2", tag="acc")
@@ -254,7 +287,7 @@ def tile_sympnetgradientshearblock_x1_kernel(tc, p, q, k, d, e, b, a, out, out_w
                 nc.tensor.transpose(bank[:, t, :], rt[g, n, s][:, t * P : (t + 1) * P], ident32[:])
 
         def add(g, n, s):
-            if s == 0:
+            if (g, n) not in ot:
                 ot[g, n] = o_pool.tile([P, 4, W], F32, name="ot", tag="ot", align_bytes=64)
             bank = rbank[g, n, s]
             c0 = n * W + s * P
@@ -262,11 +295,40 @@ def tile_sympnetgradientshearblock_x1_kernel(tc, p, q, k, d, e, b, a, out, out_w
                 out=ot[g, n][:, :, s * P : (s + 1) * P], in0=bank[:], in1=p_sb[g][:, :, c0 : c0 + P], op=ALU.add
             )
 
+        def mmA(g, n, t):
+            acc = acc2[g, n, t] = acc_psum.tile([P, W], F32, name="acc2", tag="acc")
+            cols = slice(t * P, (t + 1) * P)
+            for gf in range(GF):
+                nc.tensor.matmul_mx(
+                    out=acc[:],
+                    lhsT=gc[g, gf][:, cols].bitcast(FP8X4),
+                    lhsT_scale=gs[g, gf][:, cols],
+                    rhs=ktc[n, gf][:].bitcast(FP8X4),
+                    rhs_scale=kts[n, gf][:],
+                    start=(gf == 0),
+                    stop=(gf == GF - 1),
+                )
+
+        def rdA(g, n, t):
+            if (g, n) not in t1:
+                t1[g, n] = t1_pool.tile([P, 4, W], F32, name="t1", tag="t1", align_bytes=64)
+            nc.vector.tensor_tensor(
+                out=t1[g, n][:, t, :], in0=acc2[g, n, t][:], in1=d_all[:, n * W : (n + 1) * W], op=ALU.mult
+            )
+
+        def addA(g, n, t0, t1_, eng):
+            if (g, n) not in ot:
+                ot[g, n] = o_pool.tile([P, 4, W], F32, name="ot", tag="ot", align_bytes=64)
+            e_ = nc.vector if eng == "V" else nc.gpsimd
+            e_.tensor_tensor(
+                out=ot[g, n][:, t0:t1_, :], in0=t1[g, n][:, t0:t1_, :], in1=p_sb[g][:, t0:t1_, n * W : (n + 1) * W], op=ALU.add
+            )
+
         def ob_(g, n, c0, c1, eng="S"):
             if (g, n) not in ob:
                 ob[g, n] = grp_pool.tile([P, W, 4], BF16, name="ob", tag="grp", align_bytes=64)
-            dst = ob[g, n][:, c0:c1, :]
-            src = ot[g, n][:, :, c0:c1].rearrange("p t n -> p n t")
+            dst = ob[g, n][:, c0:c1, :].rearrange("p (c i) t -> p c t i", i=PAIR)
+            src = ot[g, n][:, :, c0:c1].rearrange("p t (c i) -> p c t i", i=PAIR)
             if eng == "S":
                 nc.scalar.copy(dst, src)
             else:
@@ -283,8 +345,8 @@ def tile_sympnetgradientshearblock_x1_kernel(tc, p, q, k, d, e, b, a, out, out_w
                 in_=ob[g, n][:, c0:c1, :].rearrange("p n t -> p (n t)"),
             )
 
-        def st_o(g, n):
-            nc.sync.dma_start(out=out4[g, :, :, n * W : (n + 1) * W], in_=ot[g, n][:])
+        def st_o(g, n, c0=0, c1=W):
+            nc.sync.dma_start(out=out4[g, :, :, n * W + c0 : n * W + c1], in_=ot[g, n][:, :, c0:c1])
 
         def st_w(g, n, c0, c1):
             nc.sync.dma_start(
@@ -297,157 +359,167 @@ def tile_sympnetgradientshearblock_x1_kernel(tc, p, q, k, d, e, b, a, out, out_w
                 nc.sync.dma_start(
                     out=out_scales[g, 4 * qd : 4 * qd + 4, :].bitcast(I32), in_=osc[g][32 * qd : 32 * qd + 4, :].bitcast(I32)
                 )
-        vectors()
-        vec_cp()
-        k_il(0, 0, "S")
-        u_tr(0, 0)
-        u_mul(0, 0)
-        u_tr(0, 1)
-        u_mul(0, 1)
-        u_q(0, 0)
-        u_q(0, 1)
+        k_il(1, 0, "G")
         kt_tr(0, 0)
+        vectors()
+        k_il(0, 0, "V")
         kt_cp(0, 0)
-        k_il(1, 0, "S")
-        k_il(0, 1, "V")
-        k_il(1, 1, "S")
-        k_q(0, 0)
-        k_q(1, 0)
-        u_tr(1, 0)
-        u_mul(1, 0)
-        mm1(0, 0)
+        u_tr(0, 0)
         kt_q(0, 0)
-        k_q(0, 1)
-        k_q(1, 1)
-        k_il(0, 2, "V")
-        tanh(0, 0)
-        k_il(1, 2, "S")
+        u_tr(0, 1)
+        vec_cp()
+        u_mul(0, 0)
+        u_mul(0, 1)
+        kt_tr(1, 0)
+        k_q(0)
+        dcol()
+        kt_tr(0, 2)
+        kt_cp(1, 0)
+        u_q(0)
+        dcol_cp()
+        mm1(0, 0)
+        k_il(1, 1, "V")
+        k_il(0, 1, "S")
+        kt_cp(0, 2)
+        kt_q(1, 0)
+        k_il(1, 2, "G")
+        u_tr(1, 0)
         u_tr(1, 1)
+        k_il(0, 2, "S")
+        k_q(1)
+        kt_q(0, 2)
+        u_mul(1, 0)
         u_mul(1, 1)
+        k_q(2)
         mm1(0, 1)
-        u_q(1, 0)
-        k_q(0, 2)
-        k_q(1, 2)
+        tanh(0, 0)
         tanh(0, 1)
         am(0, 0)
-        kt_tr(0, 1)
-        kt_cp(0, 1)
-        u_q(1, 1)
-        mm1(0, 2)
-        am(0, 1)
-        gq(0, 0)
-        tanh(0, 2)
-        kt_tr(0, 2)
-        kt_cp(0, 2)
-        gq(0, 1)
-        kt_q(0, 1)
-        am(0, 2)
-        mm1(1, 0)
-        kt_q(0, 2)
-        gq(0, 2)
-        kt_tr(1, 0)
-        kt_cp(1, 0)
+        u_q(1)
         kt_tr(1, 1)
+        mm1(0, 2)
+        mm1(1, 0)
+        am(0, 1)
         kt_cp(1, 1)
-        kt_q(1, 0)
-        tanh(1, 0)
-        dcol()
-        kt_tr(1, 2)
-        dcol_cp()
+        tanh(0, 2)
+        gq(0, 0)
+        kt_tr(0, 1)
         kt_q(1, 1)
-        kt_cp(1, 2)
+        am(0, 2)
+        tanh(1, 0)
+        kt_cp(0, 1)
         am(1, 0)
-        kt_q(1, 2)
-        gq(1, 0)
-        mm2(0, 0, 0)
-        rd(0, 0, 0)
-        mm2(0, 0, 1)
-        rd(0, 0, 1)
-        mm2(0, 0, 2)
-        rd(0, 0, 2)
-        mm2(0, 0, 3)
-        rd(0, 0, 3)
+        kt_q(0, 1)
         mm1(1, 1)
+        kt_tr(1, 2)
+        gq(0, 1)
+        gq(0, 2)
         tanh(1, 1)
-        rtr(0, 0, 0)
-        add(0, 0, 0)
-        rtr(0, 0, 1)
-        add(0, 0, 1)
-        mm1(1, 2)
         am(1, 1)
+        mm1(1, 2)
         tanh(1, 2)
-        rtr(0, 0, 2)
-        add(0, 0, 2)
-        rtr(0, 0, 3)
-        add(0, 0, 3)
-        st_o(0, 0)
-        gq(1, 1)
-        mm2(0, 1, 0)
-        rd(0, 1, 0)
+        mm2(0, 0, 2)
+        kt_cp(1, 2)
+        gq(1, 0)
+        kt_q(1, 2)
+        mm2(0, 0, 1)
+        mm2(0, 0, 0)
+        mm2(0, 0, 3)
         mm2(0, 1, 1)
-        rd(0, 1, 1)
-        mm2(0, 1, 2)
-        rd(0, 1, 2)
-        mm2(0, 1, 3)
-        rd(0, 1, 3)
+        rd(0, 0, 1)
+        rd(0, 0, 2)
         am(1, 2)
-        ob_(0, 0, 0, 512)
-        gq(1, 2)
-        rtr(0, 1, 0)
-        add(0, 1, 0)
+        rd(0, 0, 3)
+        rtr(0, 0, 1)
+        rtr(0, 0, 2)
+        mm2(0, 1, 3)
+        mm2(0, 1, 2)
+        add(0, 0, 1)
+        rd(0, 1, 1)
+        mm2(0, 1, 0)
+        rtr(0, 0, 3)
+        add(0, 0, 2)
         rtr(0, 1, 1)
+        gq(1, 1)
+        rd(0, 0, 0)
+        rtr(0, 0, 0)
+        gq(1, 2)
+        add(0, 0, 3)
+        rd(0, 1, 3)
+        mm2(1, 1, 1)
+        ob_(0, 0, 128, 256, "S")
+        ob_(0, 0, 256, 384, "S")
+        mm2(1, 1, 0)
+        rd(0, 1, 0)
+        rd(0, 1, 2)
+        ob_(0, 0, 384, 512, "S")
         add(0, 1, 1)
-        rtr(0, 1, 2)
-        add(0, 1, 2)
         rtr(0, 1, 3)
+        rtr(0, 1, 0)
+        add(0, 0, 0)
+        rtr(0, 1, 2)
+        st_o(0, 0)
+        rd(1, 1, 1)
         add(0, 1, 3)
+        rd(1, 1, 0)
+        mm2(1, 0, 1)
+        add(0, 1, 2)
+        add(0, 1, 0)
+        ob_(0, 0, 0, 128, "S")
         st_o(0, 1)
+        rd(1, 0, 1)
+        mm2(1, 1, 2)
+        rtr(1, 1, 1)
+        ob_(0, 1, 384, 512, "S")
+        ob_(0, 1, 256, 384, "S")
+        ob_(0, 1, 0, 128, "S")
         oq(0, 0, 0, 512)
+        rtr(1, 1, 0)
+        rd(1, 1, 2)
+        rtr(1, 0, 1)
+        ob_(0, 1, 128, 256, "V")
+        mm2(1, 1, 3)
+        mm2(1, 0, 2)
+        add(1, 1, 0)
+        add(1, 1, 1)
+        oq(0, 1, 0, 512)
+        rd(1, 0, 2)
         st_w(0, 0, 0, 512)
         mm2(1, 0, 0)
-        rd(1, 0, 0)
-        mm2(1, 0, 1)
-        rd(1, 0, 1)
-        mm2(1, 0, 2)
-        rd(1, 0, 2)
-        mm2(1, 0, 3)
-        rd(1, 0, 3)
-        ob_(0, 1, 0, 512)
-        rtr(1, 0, 0)
-        add(1, 0, 0)
-        rtr(1, 0, 1)
-        add(1, 0, 1)
-        rtr(1, 0, 2)
-        add(1, 0, 2)
-        rtr(1, 0, 3)
-        add(1, 0, 3)
-        st_o(1, 0)
-        oq(0, 1, 0, 512)
-        st_w(0, 1, 0, 512)
-        st_s(0)
-        mm2(1, 1, 0)
-        rd(1, 1, 0)
-        mm2(1, 1, 1)
-        rd(1, 1, 1)
-        mm2(1, 1, 2)
-        rd(1, 1, 2)
-        mm2(1, 1, 3)
-        rd(1, 1, 3)
-        ob_(1, 0, 0, 512)
-        rtr(1, 1, 0)
-        add(1, 1, 0)
-        rtr(1, 1, 1)
-        add(1, 1, 1)
         rtr(1, 1, 2)
+        add(1, 0, 1)
+        st_w(0, 1, 0, 512)
+        rd(1, 1, 3)
+        ob_(1, 1, 128, 256, "S")
+        rtr(1, 0, 2)
         add(1, 1, 2)
         rtr(1, 1, 3)
+        add(1, 0, 2)
+        mm2(1, 0, 3)
+        rd(1, 0, 0)
+        st_s(0)
+        rd(1, 0, 3)
+        ob_(1, 1, 256, 384, "S")
         add(1, 1, 3)
-        st_o(1, 1)
+        ob_(1, 0, 128, 256, "S")
+        rtr(1, 0, 0)
+        add(1, 0, 0)
+        ob_(1, 1, 0, 128, "S")
+        st_o(1, 1, 0, 256)
+        rtr(1, 0, 3)
+        add(1, 0, 3)
+        st_o(1, 1, 256, 512)
+        ob_(1, 1, 384, 512, "V")
+        ob_(1, 0, 384, 512, "V")
+        ob_(1, 0, 256, 384, "S")
+        ob_(1, 0, 0, 128, "V")
+        oq(1, 1, 128, 256)
+        oq(1, 1, 384, 512)
         oq(1, 0, 0, 512)
+        st_o(1, 0)
         st_w(1, 0, 0, 512)
-        ob_(1, 1, 0, 256)
-        ob_(1, 1, 256, 512, "V")
-        oq(1, 1, 256, 512)
-        oq(1, 1, 0, 256)
-        st_w(1, 1, 0, 512)
+        oq(1, 1, 0, 128)
+        oq(1, 1, 256, 384)
         st_s(1)
+        st_w(1, 1, 0, 256)
+        st_w(1, 1, 256, 512)

from contextlib import ExitStack

import concourse.mybir as mybir
from concourse.masks import make_identity

N, D, F = 1024, 1024, 1536
FLOPS = 2 * 2 * N * D * F

F32 = mybir.dt.float32
BF16 = mybir.dt.bfloat16
I32 = mybir.dt.int32
U32 = mybir.dt.uint32
U8 = mybir.dt.uint8
FP8X4 = mybir.dt.float8_e4m3fn_x4
ACT = mybir.ActivationFunctionType
ALU = mybir.AluOpType

P = 128
TG = 2
GD = 2
GF = 3
W = 512
PAIR = 2


def tile_sympnetgradientshearblock_x1_kernel(tc, p, q, k, d, e, b, a, out, out_words, out_scales):
    nc = tc.nc
    ctx = ExitStack()
    with ctx:
        keep = ctx.enter_context(tc.tile_pool(name="keep", bufs=1))
        grp_pool = ctx.enter_context(tc.tile_pool(name="grp", bufs=5))
        grp2_pool = ctx.enter_context(tc.tile_pool(name="grp2", bufs=4))
        th_pool = ctx.enter_context(tc.tile_pool(name="th", bufs=2))
        o_pool = ctx.enter_context(tc.tile_pool(name="o", bufs=3))
        oc_pool = ctx.enter_context(tc.tile_pool(name="oc", bufs=3))
        t1_pool = ctx.enter_context(tc.tile_pool(name="t1", bufs=2))
        rt_pool = ctx.enter_context(tc.tile_pool(name="rt", bufs=4))
        tr_psum = ctx.enter_context(tc.psum_pool(name="trp", bufs=3))
        acc_psum = ctx.enter_context(tc.psum_pool(name="accp", bufs=8 - 3))
        if True:
            ctx.enter_context(tc.manual_schedule())

        q4 = q.rearrange("(g m t) x -> g m t x", g=TG, t=4)
        p4 = p.rearrange("(g m t) x -> g m t x", g=TG, t=4)
        out4 = out.rearrange("(g m t) x -> g m t x", g=TG, t=4)
        k4 = k.rearrange("(g m j) f -> g m j f", g=GD, j=4)

        vec = keep.tile([P, W], BF16, name="vec", align_bytes=64)
        nc.gpsimd.memset(vec[:], 0.0)
        warm = keep.tile([P, 1], F32, name="warm")
        nc.vector.memset(warm[:], 0.0)
        ident32 = keep.tile([P, P], F32, name="ident32", align_bytes=64)
        make_identity(nc, ident32[:])
        ident16 = keep.tile([P, P], BF16, name="ident16", align_bytes=64)
        nc.vector.tensor_copy(out=ident16[:], in_=ident32[:])

        q_sb, k_sb, p_sb = {}, {}, {}

        def load_q(g, t0, t1):
            tile = keep.tile([P, t1 - t0, D], BF16, name="q%d%d" % (g, t0), align_bytes=64)
            nc.sync.dma_start(out=tile[:], in_=q4[g, :, t0:t1, :])
            for t in range(t0, t1):
                q_sb[g, t] = tile[:, t - t0, :]

        def load_k(gd, f0, f1):
            tile = keep.tile([P, 4, (f1 - f0) * W], BF16, name="k%d%d" % (gd, f0), align_bytes=64)
            nc.sync.dma_start(out=tile[:], in_=k4[gd, :, :, f0 * W : f1 * W])
            for gf in range(f0, f1):
                k_sb[gd, gf] = tile[:, :, (gf - f0) * W : (gf - f0 + 1) * W]

        def load_p(g):
            p_sb[g] = keep.tile([P, 4, D], BF16, name="p%d" % g, align_bytes=64)
            nc.sync.dma_start(out=p_sb[g][:], in_=p4[g])

        load_k(0, 0, 1)
        for row, (v, n) in ((9, (d, GD)), (0, (e, GF)), (3, (b, GF)), (6, (a, GF))):
            nc.sync.dma_start(out=vec[row : row + n, :], in_=v.rearrange("(g x) -> g x", g=n))
        load_q(0, 0, 2)
        load_k(1, 0, 1)
        load_q(0, 2, 4)
        load_k(0, 1, 3)
        load_k(1, 1, 3)
        load_q(1, 0, 4)
        load_p(0)
        load_p(1)

        nc.scalar.activation(warm[:], warm[:], ACT.Tanh)

        a4 = keep.tile([P, GF, 4], F32, name="a4")
        eb = keep.tile([P, 4, 6], F32, name="eb")
        d4 = keep.tile([P, GD, 4], BF16, name="d4")

        vps = {}

        def vectors():
            ps = tr_psum.tile([P, 4, P], BF16, name="vps", tag="tr")
            for t in range(4):
                nc.tensor.transpose(ps[:, t, :], vec[:, t : W : 4], ident16[:])
            vps[0] = ps

        def vec_cp():
            ps = vps[0]
            nc.vector.tensor_copy(out=d4[:], in_=ps[:, :, 9:11].rearrange("p t g -> p g t"))
            nc.vector.tensor_copy(out=a4[:], in_=ps[:, :, 6:9].rearrange("p t g -> p g t"))
            nc.vector.tensor_copy(out=eb[:], in_=ps[:, :, 0:6])

        d_col = keep.tile([P, 8], F32, name="d_col")

        d_all = keep.tile([P, D], BF16, name="d_all", align_bytes=64)

        def dsp():
            ps = vps[2] = tr_psum.tile([P, GD, 4, P], BF16, name="dps", tag="tr")
            for g in range(GD):
                for t in range(4):
                    nc.tensor.transpose(ps[:, g, t, :], d4[:, g, t : t + 1].to_broadcast([P, P]), ident16[:])

        def dsp_cp():
            nc.scalar.copy(d_all[:].rearrange("p (g m t) -> p g m t", g=GD, t=4), vps[2][:].rearrange("p g t m -> p g m t"))

        def dcol():
            ps = tr_psum.tile([P, 4, P], BF16, name="dps", tag="tr")
            for s in range(4):
                nc.tensor.transpose(ps[:, s, :], vec[:, s * P : (s + 1) * P], ident16[:])
            vps[1] = ps

        def dcol_cp():
            ps = vps[1]
            nc.vector.tensor_copy(out=d_col[:].rearrange("p (g s) -> p g s", g=GD), in_=ps[:, :, 9:11].rearrange("p s g -> p g s"))

        ug, uc, us = {}, {}, {}

        ubank = {}

        def u_tr(g, pair):
            for gd in range(GD):
                if (g, 0) not in ug:
                    tile = grp2_pool.tile([P, GD, W, 4], BF16, name="ug", tag="grp2", align_bytes=64)
                    ug[g] = tile
                    for x in range(GD):
                        ug[g, x] = tile[:, x, :, :]
                bank = ubank[g, pair, gd] = tr_psum.tile([P, 2, 2, P], F32, name="ubank", tag="tr")
                for u in range(2):
                    for tt in range(2):
                        words = q_sb[g, 2 * pair + tt].bitcast(F32)
                        nc.tensor.transpose(bank[:, u, tt, :], words[:, 256 * gd + u : 256 * (gd + 1) : 2], ident32[:])

        def u_mul(g, pair):
            for gd in range(GD):
                bank = ubank[g, pair, gd]
                nc.vector.tensor_tensor(
                    out=ug[g, gd][:, 256 * pair : 256 * (pair + 1), :].rearrange("p n (u e) -> p n u e", e=2),
                    in0=bank[:].rearrange("p u t m -> p (u t m)").bitcast(BF16).rearrange("p (u n e) -> p n u e", u=2, e=2),
                    in1=d4[:, gd, :].rearrange("p (u e) -> p u e", e=2).unsqueeze(1).to_broadcast([P, 256, 2, 2]),
                    op=ALU.mult,
                )

        def quant(src, name):
            codes = keep.tile([P, W], U32, name=name + "c", align_bytes=64)
            scales = keep.tile([P, W], U8, name=name + "s", align_bytes=64)
            nc.vector.quantize_mx(out=codes[:].bitcast(FP8X4), scales=scales[:], in_=src[:].rearrange("p n t -> p (n t)"))
            return codes, scales

        def quant2(src, name):
            codes = keep.tile([P, GD, W], U32, name=name + "c", align_bytes=64)
            scales = keep.tile([P, GD, W], U8, name=name + "s", align_bytes=64)
            nc.vector.quantize_mx(
                out=codes[:].rearrange("p g n -> p (g n)").bitcast(FP8X4),
                scales=scales[:].rearrange("p g n -> p (g n)"),
                in_=src[:].rearrange("p g n t -> p (g n t)"),
            )
            return codes, scales

        def u_q(g):
            codes, scales = quant2(ug[g], "u%d" % g)
            for gd in range(GD):
                uc[g, gd], us[g, gd] = codes[:, gd, :], scales[:, gd, :]

        kg, kc, ks = {}, {}, {}

        def k_il(gd, gf, eng):
            if gf not in kg:
                kg[gf] = grp2_pool.tile([P, GD, W, 4], BF16, name="kg", tag="grp2", align_bytes=64)
            dst = kg[gf][:, gd, :, :].rearrange("p (t m) j -> p t m j", t=4)
            src = k_sb[gd, gf].rearrange("p j (m t) -> p t m j", t=4)
            if eng == "V":
                nc.vector.tensor_copy(out=dst, in_=src)
            elif eng == "G":
                nc.gpsimd.tensor_scalar(out=dst, in0=src, scalar1=1.0, scalar2=0.0, op0=ALU.mult, op1=ALU.add)
            else:
                nc.scalar.copy(dst, src)

        def k_q(gf):
            codes, scales = quant2(kg[gf], "k%d" % gf)
            for gd in range(GD):
                kc[gd, gf], ks[gd, gf] = codes[:, gd, :], scales[:, gd, :]

        ktg, ktc, kts = {}, {}, {}

        kbank = {}

        def kt_tr(gd, gf):
            for jj in range(2):
                bank = kbank[gd, gf, jj] = tr_psum.tile([P, 2, 2, P], F32, name="kbank", tag="tr")
                for j in range(2):
                    words = k_sb[gd, gf][:, 2 * jj + j, :].bitcast(F32)
                    for u in range(2):
                        nc.tensor.transpose(bank[:, j, u, :], words[:, u : 256 : 2], ident32[:])

        def kt_cp(gd, gf, eng="S"):
            ktg[gd, gf] = grp_pool.tile([P, W, 4], BF16, name="ktg", tag="grp", align_bytes=64)
            dst = ktg[gd, gf][:].rearrange("p n t -> p (n t)").bitcast(F32).rearrange("p (m j u) -> p m j u", j=4, u=2)
            for jj in range(2):
                src = kbank[gd, gf, jj][:].rearrange("p j u m -> p m j u")
                if eng == "S":
                    nc.scalar.copy(dst[:, :, 2 * jj : 2 * jj + 2, :], src)
                else:
                    nc.vector.tensor_copy(out=dst[:, :, 2 * jj : 2 * jj + 2, :], in_=src)

        def kt_q(gd, gf):
            ktc[gd, gf], kts[gd, gf] = quant(ktg[gd, gf], "kt%d%d" % (gd, gf))

        th, gg, gc, gs = {}, {}, {}, {}

        acc1 = {}

        def mm1(g, gf):
            for t in range(4):
                acc = acc1[g, gf, t] = acc_psum.tile([P, W], F32, name="acc1", tag="acc")
                cols = slice(t * P, (t + 1) * P)
                for gd in range(GD):
                    nc.tensor.matmul_mx(
                        out=acc[:],
                        lhsT=kc[gd, gf][:, cols].bitcast(FP8X4),
                        lhsT_scale=ks[gd, gf][:, cols],
                        rhs=uc[g, gd].bitcast(FP8X4),
                        rhs_scale=us[g, gd],
                        start=(gd == 0),
                        stop=(gd == GD - 1),
                    )

        def tanh(g, gf):
            th[g, gf] = th_pool.tile([P, 4, W], F32, name="th", tag="th", align_bytes=64)
            for t in range(4):
                acc = acc1[g, gf, t]
                nc.scalar.activation(
                    th[g, gf][:, t, :], acc[:], ACT.Tanh, bias=eb[:, t, 3 + gf : 4 + gf], scale=eb[:, t, gf : gf + 1]
                )

        def am(g, gf):
            gg[g, gf] = grp_pool.tile([P, W, 4], BF16, name="gg", tag="grp", align_bytes=64)
            nc.vector.tensor_tensor(
                out=gg[g, gf][:].rearrange("p (c i) t -> p c t i", i=PAIR),
                in0=th[g, gf][:].rearrange("p t (c i) -> p c t i", i=PAIR),
                in1=a4[:, gf, :].unsqueeze(1).unsqueeze(3).to_broadcast([P, W // PAIR, 4, PAIR]),
                op=ALU.mult,
            )

        def gq(g, gf):
            gc[g, gf], gs[g, gf] = quant(gg[g, gf], "g%d%d" % (g, gf))

        ot, ob, oc, osc = {}, {}, {}, {}

        rt, acc2, rbank, t1 = {}, {}, {}, {}

        def mm2(g, n, s):
            acc = acc2[g, n, s] = acc_psum.tile([P, W], F32, name="acc2", tag="acc")
            cols = slice(s * P, (s + 1) * P)
            for gf in range(GF):
                nc.tensor.matmul_mx(
                    out=acc[:],
                    lhsT=ktc[n, gf][:, cols].bitcast(FP8X4),
                    lhsT_scale=kts[n, gf][:, cols],
                    rhs=gc[g, gf][:].bitcast(FP8X4),
                    rhs_scale=gs[g, gf][:],
                    start=(gf == 0),
                    stop=(gf == GF - 1),
                )

        def rd(g, n, s):
            acc = acc2[g, n, s]
            rt[g, n, s] = rt_pool.tile([P, W], F32, name="rt", tag="rt", align_bytes=64)
            nc.scalar.activation(rt[g, n, s][:], acc[:], ACT.Copy, scale=d_col[:, n * 4 + s : n * 4 + s + 1])

        def rtr(g, n, s):
            bank = rbank[g, n, s] = tr_psum.tile([P, 4, P], F32, name="rbank", tag="tr")
            for t in range(4):
                nc.tensor.transpose(bank[:, t, :], rt[g, n, s][:, t * P : (t + 1) * P], ident32[:])

        def add(g, n, s):
            if (g, n) not in ot:
                ot[g, n] = o_pool.tile([P, 4, W], F32, name="ot", tag="ot", align_bytes=64)
            bank = rbank[g, n, s]
            c0 = n * W + s * P
            nc.vector.tensor_tensor(
                out=ot[g, n][:, :, s * P : (s + 1) * P], in0=bank[:], in1=p_sb[g][:, :, c0 : c0 + P], op=ALU.add
            )

        def mmA(g, n, t):
            acc = acc2[g, n, t] = acc_psum.tile([P, W], F32, name="acc2", tag="acc")
            cols = slice(t * P, (t + 1) * P)
            for gf in range(GF):
                nc.tensor.matmul_mx(
                    out=acc[:],
                    lhsT=gc[g, gf][:, cols].bitcast(FP8X4),
                    lhsT_scale=gs[g, gf][:, cols],
                    rhs=ktc[n, gf][:].bitcast(FP8X4),
                    rhs_scale=kts[n, gf][:],
                    start=(gf == 0),
                    stop=(gf == GF - 1),
                )

        def rdA(g, n, t):
            if (g, n) not in t1:
                t1[g, n] = t1_pool.tile([P, 4, W], F32, name="t1", tag="t1", align_bytes=64)
            nc.vector.tensor_tensor(
                out=t1[g, n][:, t, :], in0=acc2[g, n, t][:], in1=d_all[:, n * W : (n + 1) * W], op=ALU.mult
            )

        def addA(g, n, t0, t1_, eng):
            if (g, n) not in ot:
                ot[g, n] = o_pool.tile([P, 4, W], F32, name="ot", tag="ot", align_bytes=64)
            e_ = nc.vector if eng == "V" else nc.gpsimd
            e_.tensor_tensor(
                out=ot[g, n][:, t0:t1_, :], in0=t1[g, n][:, t0:t1_, :], in1=p_sb[g][:, t0:t1_, n * W : (n + 1) * W], op=ALU.add
            )

        def ob_(g, n, c0, c1, eng="S"):
            if (g, n) not in ob:
                ob[g, n] = grp_pool.tile([P, W, 4], BF16, name="ob", tag="grp", align_bytes=64)
            dst = ob[g, n][:, c0:c1, :].rearrange("p (c i) t -> p c t i", i=PAIR)
            src = ot[g, n][:, :, c0:c1].rearrange("p t (c i) -> p c t i", i=PAIR)
            if eng == "S":
                nc.scalar.copy(dst, src)
            else:
                nc.vector.tensor_copy(out=dst, in_=src)

        def oq(g, n, c0, c1):
            if (g, n) not in oc:
                oc[g, n] = oc_pool.tile([P, W], U32, name="oc", tag="oc", align_bytes=64)
                if g not in osc:
                    osc[g] = keep.tile([P, D], U8, name="osc%d" % g, align_bytes=64)
            nc.vector.quantize_mx(
                out=oc[g, n][:, c0:c1].bitcast(FP8X4),
                scales=osc[g][:, n * W + c0 : n * W + c1],
                in_=ob[g, n][:, c0:c1, :].rearrange("p n t -> p (n t)"),
            )

        def st_o(g, n, c0=0, c1=W):
            nc.sync.dma_start(out=out4[g, :, :, n * W + c0 : n * W + c1], in_=ot[g, n][:, :, c0:c1])

        def st_w(g, n, c0, c1):
            nc.sync.dma_start(
                out=out_words[g, :, n * W + c0 : n * W + c1, :].rearrange("p m t -> p (m t)").bitcast(I32),
                in_=oc[g, n][:, c0:c1].bitcast(I32),
            )

        def st_s(g):
            for qd in range(4):
                nc.sync.dma_start(
                    out=out_scales[g, 4 * qd : 4 * qd + 4, :].bitcast(I32), in_=osc[g][32 * qd : 32 * qd + 4, :].bitcast(I32)
                )
        k_il(1, 0, "G")
        kt_tr(0, 0)
        vectors()
        k_il(0, 0, "V")
        kt_cp(0, 0)
        u_tr(0, 0)
        kt_q(0, 0)
        u_tr(0, 1)
        vec_cp()
        u_mul(0, 0)
        u_mul(0, 1)
        kt_tr(1, 0)
        k_q(0)
        dcol()
        kt_tr(0, 2)
        kt_cp(1, 0)
        u_q(0)
        dcol_cp()
        mm1(0, 0)
        k_il(1, 1, "V")
        k_il(0, 1, "S")
        kt_cp(0, 2)
        kt_q(1, 0)
        k_il(1, 2, "G")
        u_tr(1, 0)
        u_tr(1, 1)
        k_il(0, 2, "S")
        k_q(1)
        kt_q(0, 2)
        u_mul(1, 0)
        u_mul(1, 1)
        k_q(2)
        mm1(0, 1)
        tanh(0, 0)
        tanh(0, 1)
        am(0, 0)
        u_q(1)
        kt_tr(1, 1)
        mm1(0, 2)
        mm1(1, 0)
        am(0, 1)
        kt_cp(1, 1)
        tanh(0, 2)
        gq(0, 0)
        kt_tr(0, 1)
        kt_q(1, 1)
        am(0, 2)
        tanh(1, 0)
        kt_cp(0, 1)
        am(1, 0)
        kt_q(0, 1)
        mm1(1, 1)
        kt_tr(1, 2)
        gq(0, 1)
        gq(0, 2)
        tanh(1, 1)
        am(1, 1)
        mm1(1, 2)
        tanh(1, 2)
        mm2(0, 0, 2)
        kt_cp(1, 2)
        gq(1, 0)
        kt_q(1, 2)
        mm2(0, 0, 1)
        mm2(0, 0, 0)
        mm2(0, 0, 3)
        mm2(0, 1, 1)
        rd(0, 0, 1)
        rd(0, 0, 2)
        am(1, 2)
        rd(0, 0, 3)
        rtr(0, 0, 1)
        rtr(0, 0, 2)
        mm2(0, 1, 3)
        mm2(0, 1, 2)
        add(0, 0, 1)
        rd(0, 1, 1)
        mm2(0, 1, 0)
        rtr(0, 0, 3)
        add(0, 0, 2)
        rtr(0, 1, 1)
        gq(1, 1)
        rd(0, 0, 0)
        rtr(0, 0, 0)
        gq(1, 2)
        add(0, 0, 3)
        rd(0, 1, 3)
        mm2(1, 1, 1)
        ob_(0, 0, 128, 256, "S")
        ob_(0, 0, 256, 384, "S")
        mm2(1, 1, 0)
        rd(0, 1, 0)
        rd(0, 1, 2)
        ob_(0, 0, 384, 512, "S")
        add(0, 1, 1)
        rtr(0, 1, 3)
        rtr(0, 1, 0)
        add(0, 0, 0)
        rtr(0, 1, 2)
        st_o(0, 0)
        rd(1, 1, 1)
        add(0, 1, 3)
        rd(1, 1, 0)
        mm2(1, 0, 1)
        add(0, 1, 2)
        add(0, 1, 0)
        ob_(0, 0, 0, 128, "S")
        st_o(0, 1)
        rd(1, 0, 1)
        mm2(1, 1, 2)
        rtr(1, 1, 1)
        ob_(0, 1, 384, 512, "S")
        ob_(0, 1, 256, 384, "S")
        ob_(0, 1, 0, 128, "S")
        oq(0, 0, 0, 512)
        rtr(1, 1, 0)
        rd(1, 1, 2)
        rtr(1, 0, 1)
        ob_(0, 1, 128, 256, "V")
        mm2(1, 1, 3)
        mm2(1, 0, 2)
        add(1, 1, 0)
        add(1, 1, 1)
        oq(0, 1, 0, 512)
        rd(1, 0, 2)
        st_w(0, 0, 0, 512)
        mm2(1, 0, 0)
        rtr(1, 1, 2)
        add(1, 0, 1)
        st_w(0, 1, 0, 512)
        rd(1, 1, 3)
        ob_(1, 1, 128, 256, "S")
        rtr(1, 0, 2)
        add(1, 1, 2)
        rtr(1, 1, 3)
        add(1, 0, 2)
        mm2(1, 0, 3)
        rd(1, 0, 0)
        st_s(0)
        rd(1, 0, 3)
        ob_(1, 1, 256, 384, "S")
        add(1, 1, 3)
        ob_(1, 0, 128, 256, "S")
        rtr(1, 0, 0)
        add(1, 0, 0)
        ob_(1, 1, 0, 128, "S")
        st_o(1, 1, 0, 256)
        rtr(1, 0, 3)
        add(1, 0, 3)
        st_o(1, 1, 256, 512)
        ob_(1, 1, 384, 512, "V")
        ob_(1, 0, 384, 512, "V")
        ob_(1, 0, 256, 384, "S")
        ob_(1, 0, 0, 128, "V")
        oq(1, 1, 128, 256)
        oq(1, 1, 384, 512)
        oq(1, 0, 0, 512)
        st_o(1, 0)
        st_w(1, 0, 0, 512)
        oq(1, 1, 0, 128)
        oq(1, 1, 256, 384)
        st_s(1)
        st_w(1, 1, 0, 256)
        st_w(1, 1, 256, 512)
